import numpy as np
import ml_dtypes


def mxq(x, axis, fmt="e4m3"):
    dtype, down = {"e4m3": (ml_dtypes.float8_e4m3fn, 7), "e5m2": (ml_dtypes.float8_e5m2, 14)}[fmt]
    v = np.moveaxis(np.asarray(x, np.float32).astype(ml_dtypes.bfloat16).astype(np.float64), axis, -1)
    blocks = v.reshape(v.shape[:-1] + (-1, 32))
    amax = np.abs(blocks).max(-1, keepdims=True)
    byte = np.maximum(np.where(amax > 0, np.frexp(amax)[1] - 1 + 127, 0) - down, 1)
    scale = np.exp2(byte - 127.0)
    codes = (blocks / scale).astype(np.float32).astype(dtype).astype(np.float64)
    return np.moveaxis((codes * scale).reshape(v.shape), -1, axis)


WIDE = False


def mx_kscale(k):
    if not WIDE:
        return np.ones(k)
    levels = np.array([30, -30])
    if k % 512:
        return np.exp2(np.random.permutation(np.resize(levels, k // 32))).repeat(32)
    a = np.empty((k // 512, 16))
    for p in range(k // 512):
        a[p, :8] = np.random.permutation(np.resize(levels, 8))
        for g in range(8):
            far = levels[np.abs(levels - a[p, g]) >= 10]
            a[p, g + 8] = far[np.random.randint(len(far))]
    return np.exp2(a.ravel()).repeat(32)


def f64(x):
    return np.asarray(x).astype(np.float64)


def striped(idx):
    return np.tile(np.asarray(idx).reshape(-1, 16).T, (8, 1)).astype(np.uint16)


def unstriped(offs):
    return offs[:16].T.reshape(-1).astype(np.int64)


E2M1 = np.array([0.0, 0.5, 1.0, 1.5, 2.0, 3.0, 4.0, 6.0, -0.0, -0.5, -1.0, -1.5, -2.0, -3.0, -4.0, -6.0])


def pack_weight(w, fmt):
    k, n = w.shape
    w = f64(np.asarray(w, np.float32).astype(ml_dtypes.bfloat16)).reshape(k // 32, 32, n)
    amax = np.abs(w).max(1)
    if fmt in ("e4m3", "e5m2"):
        byte = np.frexp(amax)[1] - 1 + 127 - (7 if fmt == "e4m3" else 14)
    else:
        mant, ex = np.frexp(amax / 6.0)
        byte = np.where(mant > 0.5, ex, ex - 1) + 127
    byte = np.clip(np.where(amax > 0, byte, 1), 1, 254)
    scaled = (w * np.exp2(127.0 - byte)[:, None, :]).reshape(k, n).astype(np.float32)
    by_word = np.ascontiguousarray(scaled.reshape(k // 512, 128, 4, n).transpose(0, 1, 3, 2))
    if fmt in ("e4m3", "e5m2"):
        words = by_word.astype(ml_dtypes.float8_e4m3fn if fmt == "e4m3" else ml_dtypes.float8_e5m2).view(np.uint8)
    else:
        c = by_word.astype(ml_dtypes.float4_e2m1fn).view(np.uint8) & 0xF
        words = (c[..., 0::2] | (c[..., 1::2] << 4)).reshape(k // 512, 128, 2 * n)
    return np.ascontiguousarray(words), np.ascontiguousarray(byte.astype(np.uint8).reshape(k // 512, 16, n))


def unpack_weight(words, scales, fmt):
    g, _, n = scales.shape
    words = np.ascontiguousarray(words).reshape(g, 128, n, -1)
    if fmt in ("e4m3", "e5m2"):
        vals = words.view(ml_dtypes.float8_e4m3fn if fmt == "e4m3" else ml_dtypes.float8_e5m2).astype(np.float64)
    else:
        nib = np.empty((g, 128, n, 4), np.uint8)
        nib[..., 0::2] = words & 0xF
        nib[..., 1::2] = words >> 4
        vals = E2M1[nib]
    vals = vals * np.repeat(np.exp2(scales.astype(np.float64) - 127.0), 8, axis=1)[..., None]
    return vals.transpose(0, 1, 3, 2).reshape(g * 512, n)


def sigmoid(v):
    return 1.0 / (1.0 + np.exp(-v))


def sgn(shape):
    return np.random.uniform(0.5, 2.0, shape) * np.where(np.random.standard_normal(shape) < 0, -1.0, 1.0)


K, T, J, R, F, Z, O, N, S = 512, 1024, 256, 512, 512, 1024, 128, 256, 1024


def setup_inputs():
    n = np.random.standard_normal
    idx = np.random.permutation(T)[:J]
    idx2 = np.random.permutation(Z)[:J]
    idx3 = np.random.permutation(J)[:O]
    idx4 = np.random.permutation(J)[:O]
    idx5 = np.random.permutation(J)[:O]
    idx6 = np.random.permutation(J)[:O]
    idx7 = np.random.permutation(S)[:N]
    fk = mx_kscale(K)
    ff = mx_kscale(F)
    fr = mx_kscale(R)
    xtp = pack_weight(n((K, T)) / fk[:, None], "e4m3")
    xop = pack_weight(n((F, Z)) / ff[:, None], "e2m1")
    wp = pack_weight(n((K, R)) * 1 / np.sqrt(K) * fk[:, None], "e2m1")
    w0p = pack_weight(n((F, R)) * 1 / np.sqrt(F) * ff[:, None], "e5m2")
    vsp = pack_weight(n((R, S)) * 1 / np.sqrt(R) / fr[:, None], "e5m2")
    return {
        "xt_words": xtp[0],
        "xt_scales": xtp[1],
        "xo_words": xop[0],
        "xo_scales": xop[1],
        "w_words": wp[0],
        "w_scales": wp[1],
        "w0_words": w0p[0],
        "w0_scales": w0p[1],
        "sa": (np.random.uniform(0.5, 1.6, (R, 1)) * fr[:, None]).astype(np.float32),
        "sb": (np.random.uniform(0.5, 1.6, (R, 1)) * fr[:, None]).astype(np.float32),
        "sg": (sgn((R, 1))).astype(np.float32),
        "bg": (np.random.uniform(-2.0, 2.0, (R, 1))).astype(np.float32),
        "sh": (sgn((R, 1))).astype(np.float32),
        "bh": (np.random.uniform(-2.0, 2.0, (R, 1))).astype(np.float32),
        "vs_words": vsp[0],
        "vs_scales": vsp[1],
        "offs": striped(idx),
        "offs2": striped(idx2),
        "offs3": striped(idx3),
        "offs4": striped(idx4),
        "offs5": striped(idx5),
        "offs6": striped(idx6),
        "offs7": striped(idx7),
    }


def reference(xt_words, xt_scales, xo_words, xo_scales, w_words, w_scales, w0_words, w0_scales, sa, sb, sg, bg, sh, bh, vs_words, vs_scales, offs, offs2, offs3, offs4, offs5, offs6, offs7):
    idx = unstriped(offs)
    idx2 = unstriped(offs2)
    idx3 = unstriped(offs3)
    idx4 = unstriped(offs4)
    idx5 = unstriped(offs5)
    idx6 = unstriped(offs6)
    idx7 = unstriped(offs7)
    xtu = unpack_weight(xt_words, xt_scales, "e4m3")
    xou = unpack_weight(xo_words, xo_scales, "e2m1")
    wu = unpack_weight(w_words, w_scales, "e2m1")
    w0u = unpack_weight(w0_words, w0_scales, "e5m2")
    vsu = unpack_weight(vs_words, vs_scales, "e5m2")
    xtidxg = xtu[:, idx]
    xoidx2g = xou[:, idx2]
    a = wu.T @ xtidxg + w0u.T @ xoidx2g
    u1 = a[:, idx3] * f64(sa) * sigmoid(a[:, idx4] * f64(sg) + f64(bg))
    u2 = a[:, idx5] * f64(sb) * sigmoid(a[:, idx6] * f64(sh) + f64(bh))
    hid = np.abs(u1 - u2)
    vsidx7g = vsu[:, idx7]
    hidq = mxq(hid, 0, "e4m3")
    y = vsidx7g.T @ hidq
    return y

@@ -1,0 +1,206 @@
+from contextlib import ExitStack
+
+import concourse.mybir as mybir
+
+F32 = mybir.dt.float32
+BF16 = mybir.dt.bfloat16
+I32 = mybir.dt.int32
+U32 = mybir.dt.uint32
+U16 = mybir.dt.uint16
+U8 = mybir.dt.uint8
+E4M3 = mybir.dt.float8_e4m3fn_x4
+E5M2 = mybir.dt.float8_e5m2_x4
+E2M1 = mybir.dt.float4_e2m1fn_x4
+ACT = mybir.ActivationFunctionType
+ALU = mybir.AluOpType
+
+P = 128
+PACK = 4
+QUADS = 4
+T, J, R, O, N = 1024, 256, 512, 128, 256
+FLOPS = 2 * 512 * R * J * 2 + 2 * R * N * O
+
+
+def tile_list_gatedtwins_bank_store_plain_kernel(
+    tc, xt_words, xt_scales, xo_words, xo_scales, w_words, w_scales, w0_words, w0_scales,
+    sa, sb, sg, bg, sh, bh, vs_words, vs_scales, offs, offs2, offs3, offs4, offs5, offs6, offs7, out,
+):
+    nc = tc.nc
+    with ExitStack() as ctx:
+        keep = ctx.enter_context(tc.tile_pool(name="keep", bufs=1))
+        psum = ctx.enter_context(tc.psum_pool(name="psum", bufs=1))
+
+        def new(name, shape, dtype, tag=None):
+            return keep.tile(shape, dtype, name=name, tag=tag or name, align_bytes=64)
+
+        def load_list(name, src):
+            lst = new(name, list(src.shape), U16)
+            nc.sync.dma_start(lst[:], src)
+            return lst
+
+        def zero_plane(name, width, engine):
+            plane = new(name, [P, width], U8)
+            engine.memset(plane[:].bitcast(I32), 0)
+            return plane
+
+        def load_plane(plane, scales, queue):
+            rows = scales[0].bitcast(I32)
+            for q in range(QUADS):
+                queue.dma_start(plane[:].bitcast(I32)[32 * q : 32 * q + 4, :], rows[4 * q : 4 * q + 4, :])
+
+        def load_rows(plane, scales, quads):
+            rows = scales[0].bitcast(I32)
+            for q in quads:
+                nc.sync.dma_start(plane[:].bitcast(I32)[32 * q : 32 * q + 4, :], rows[4 * q : 4 * q + 4, :])
+
+        def deal_scales(t):
+            dealt = new(f"w_sc{t}", [P, 2, P], U8)
+            nc.vector.tensor_copy(dealt[:], w_plane.rearrange("p (s q t) -> p s q t", s=2, t=PACK)[:, :, :, t])
+            return dealt
+
+        def load_stage(name, scales, queue):
+            stage = new(name, [4, QUADS, scales.shape[2] // 4], I32)
+            queue.dma_start(stage[:], scales[0].bitcast(I32).rearrange("(q r) n -> r q n", r=4))
+            return stage
+
+        def spread(plane, stage):
+            for q in range(QUADS):
+                nc.vector.tensor_copy(plane[:].bitcast(I32)[32 * q : 32 * q + 4, :], stage[:, q, :])
+
+        def load_w_stage(queue):
+            for s, scales in enumerate((w_scales, w0_scales)):
+                queue.dma_start(
+                    w_stage_words[0:4, :, s * (R // 4) : (s + 1) * (R // 4)],
+                    scales[0].bitcast(I32).rearrange("(q r) n -> r q n", r=4),
+                )
+
+        def load_vector(name, src, queue):
+            vec = new(name, [P, PACK], F32)
+            queue.dma_start(vec[:], src.rearrange("(p t) o -> p (t o)", t=PACK))
+            return vec
+
+        def load_words(name, src, dtype, queue):
+            tab = new(name, [P, src.shape[2] if dtype != U16 else src.shape[2] // 2], dtype)
+            flat = src[0] if dtype == U16 else src[0].rearrange("p n t -> p (n t)")
+            queue.dma_start(tab[:].bitcast(I32), flat.bitcast(I32))
+            return tab
+
+        def gather(name, window, lst, dtype, count):
+            got = new(name, [P, count], dtype)
+            nc.vector.tensor_copy(got[:], window.indirect(lst[:]))
+            return got
+
+        def clock(name, src):
+            tick = new(name, [P, 1], src.dtype)
+            nc.gpsimd.tensor_copy(tick[:], src)
+
+        w_stage = new("w_stage", [P, QUADS, 2 * R], U8)
+        w_stage_words = w_stage[:].bitcast(I32)
+        nc.vector.memset(w_stage_words[:, 0, :], 0)
+        w_plane = w_stage[:, 0, :]
+        xo_plane = zero_plane("xo_plane", T, nc.vector)
+        xt_plane = zero_plane("xt_plane", T, nc.vector)
+        vs_plane = zero_plane("vs_plane", T, nc.vector)
+        w_tab = load_words("w_tab", w_words, U16, nc.gpsimd)
+        w0_tab = load_words("w0_tab", w0_words, U32, nc.gpsimd)
+        l2 = load_list("l2", offs2)
+        l1 = load_list("l1", offs)
+        xo_tab = load_words("xo_tab", xo_words, U16, nc.sync)
+        load_w_stage(nc.sync)
+        load_rows(xo_plane, xo_scales, (0, 1))
+        xt_tab = load_words("xt_tab", xt_words, U32, nc.sync)
+        load_rows(xo_plane, xo_scales, (2, 3))
+        load_plane(xt_plane, xt_scales, nc.sync)
+
+        l4 = load_list("l4", offs4)
+        sg_t = load_vector("sg_t", sg, nc.sync)
+        bg_t = load_vector("bg_t", bg, nc.sync)
+        l3 = load_list("l3", offs3)
+        sa_t = load_vector("sa_t", sa, nc.sync)
+        l6 = load_list("l6", offs6)
+        sh_t = load_vector("sh_t", sh, nc.sync)
+        bh_t = load_vector("bh_t", bh, nc.sync)
+        l5 = load_list("l5", offs5)
+        sb_t = load_vector("sb_t", sb, nc.sync)
+        l7 = load_list("l7", offs7)
+        load_plane(vs_plane, vs_scales, nc.sync)
+        vs_tab = load_words("vs_tab", vs_words, U32, nc.sync)
+
+        w_all = new("w_all", [P, PACK, P], U16)
+        nc.scalar.copy(w_all[:], w_tab[:].rearrange("p (q t) -> p t q", t=PACK))
+        w0_by_t = w0_tab[:].rearrange("p (q t) -> p t q", t=PACK)
+        w0_first = new("w0_first", [P, P], U32)
+        nc.scalar.copy(w0_first[:], w0_by_t[:, 0, :])
+        w0_rest = new("w0_rest", [P, PACK - 1, P], U32)
+        nc.scalar.copy(w0_rest[:], w0_by_t[:, 1:, :])
+        w_dealt = [w_all[:, t, :] for t in range(PACK)]
+        w0_dealt = [w0_first[:]] + [w0_rest[:, t, :] for t in range(PACK - 1)]
+        for q in range(1, QUADS):
+            nc.vector.tensor_copy(w_stage_words[32 * q : 32 * q + 4, 0, :], w_stage_words[0:4, q, :])
+        w_scs = [deal_scales(0)]
+        xo_g = gather("xo_g", xo_tab[:], l2, U16, J)
+        xt_g = gather("xt_g", xt_tab[:], l1, U32, J)
+        xo_sc = gather("xo_sc", xo_plane[:], l2, U8, J)
+        xt_sc = gather("xt_sc", xt_plane[:], l1, U8, J)
+
+        a = []
+        for t in range(PACK):
+            if t == 1:
+                rest = new("w_sc_rest", [P, 2, PACK - 1, P], U8, tag="xt_plane")
+                nc.vector.tensor_copy(rest[:], w_plane.rearrange("p (s q t) -> p s t q", s=2, t=PACK)[:, :, 1:, :])
+                w_scs.extend(rest[:, :, i, :] for i in range(PACK - 1))
+            w_sc = w_scs[t]
+            acc = psum.tile([P, J], F32, name=f"acc{t}")
+            nc.tensor.matmul_mx(
+                out=acc[:], lhsT=w0_dealt[t].bitcast(E5M2), lhsT_scale=w_sc[:, 1, :],
+                rhs=xo_g[:].bitcast(E2M1), rhs_scale=xo_sc[:], start=True, stop=False,
+            )
+            nc.tensor.matmul_mx(
+                out=acc[:], lhsT=w_dealt[t].bitcast(E2M1), lhsT_scale=w_sc[:, 0, :],
+                rhs=xt_g[:].bitcast(E4M3), rhs_scale=xt_sc[:], start=False, stop=True,
+            )
+            a_t = new(f"a{t}", [P, J], F32)
+            nc.vector.tensor_copy(a_t[:], acc[:])
+            a.append(a_t)
+
+        vs_sc = gather("vs_sc", vs_plane[:], l7, U8, N)
+        vs_g = gather("vs_g", vs_tab[:], l7, U32, N)
+
+        diff = new("diff", [P, PACK, O], F32)
+        u_all = new("u_all", [P, PACK, 2, O], F32, tag="vs_tab")
+        looks = ((l4, sg_t, bg_t, l3, sa_t), (l6, sh_t, bh_t, l5, sb_t))
+        for t in range(PACK):
+            col = slice(t, t + 1)
+            gates = new(f"gates{t}", [P, 2, O], F32)
+            vals = new(f"vals{t}", [P, 2, O], F32)
+            for h, (lg, slope, offset, lv, weight) in enumerate(looks):
+                nc.scalar.activation(gates[:, h, :], a[t][:].indirect(lg[:]), ACT.Sigmoid, bias=offset[:, col], scale=slope[:, col])
+                nc.scalar.activation(vals[:, h, :], a[t][:].indirect(lv[:]), ACT.Copy, scale=weight[:, col])
+            u = u_all[:, t]
+            if t < PACK - 1:
+                nc.vector.tensor_tensor(u, vals[:], gates[:], ALU.mult)
+            else:
+                for h in range(2):
+                    nc.vector.tensor_tensor(u[:, h, :], vals[:, h, :], gates[:, h, :], ALU.mult)
+            nc.vector.tensor_tensor(diff[:, t, :], u[:, 0, :], u[:, 1, :], ALU.subtract)
+
+        hid = new("hid", [P, O, PACK], BF16)
+        woven = diff[:].rearrange("p t o -> p o t")
+        half = O // 2
+        nc.vector.scalar_tensor_tensor(hid[:, :half, :], woven[:, :half, :], -1.0, woven[:, :half, :], ALU.mult, ALU.max)
+        nc.scalar.activation(hid[:, half:, :], woven[:, half:, :], ACT.Abs)
+        hid_codes = new("hid_codes", [P, O], U32)
+        hid_sc = new("hid_sc", [P, O], U8)
+        nc.vector.quantize_mx(out=hid_codes[:].bitcast(E4M3), scales=hid_sc[:], in_=hid[:].rearrange("p o t -> p (o t)"))
+
+
+        for h, (copy, queue) in enumerate(((nc.vector.tensor_copy, nc.sync), (nc.scalar.copy, nc.scalar))):
+            cols = slice(h * P, (h + 1) * P)
+            y = psum.tile([P, O], F32, name=f"y{h}")
+            nc.tensor.matmul_mx(
+                out=y[:], lhsT=vs_g[:, cols].bitcast(E5M2), lhsT_scale=vs_sc[:, cols],
+                rhs=hid_codes[:].bitcast(E4M3), rhs_scale=hid_sc[:], start=True, stop=True,
+            )
+            y_sb = new(f"y_sb{h}", [P, O], F32)
+            copy(y_sb[:], y[:])
+            queue.dma_start(out[cols, :], y_sb[:])

@@ -94,6 +94,9 @@ def tile_list_gatedtwins_bank_store_plain_kernel(
             tick = new(name, [P, 1], src.dtype)
             nc.gpsimd.tensor_copy(tick[:], src)
 
+        warm = new("warm", [P, 2], F32)
+        nc.gpsimd.memset(warm[:, 0:1], 0.0)
+        nc.scalar.activation(warm[:, 1:2], warm[:, 0:1], ACT.Sigmoid)
         w_stage = new("w_stage", [P, QUADS, 2 * R], U8)
         w_stage_words = w_stage[:].bitcast(I32)
         nc.vector.memset(w_stage_words[:, 0, :], 0)

from contextlib import ExitStack

import concourse.mybir as mybir

F32 = mybir.dt.float32
BF16 = mybir.dt.bfloat16
I32 = mybir.dt.int32
U32 = mybir.dt.uint32
U16 = mybir.dt.uint16
U8 = mybir.dt.uint8
E4M3 = mybir.dt.float8_e4m3fn_x4
E5M2 = mybir.dt.float8_e5m2_x4
E2M1 = mybir.dt.float4_e2m1fn_x4
ACT = mybir.ActivationFunctionType
ALU = mybir.AluOpType

P = 128
PACK = 4
QUADS = 4
T, J, R, O, N = 1024, 256, 512, 128, 256
FLOPS = 2 * 512 * R * J * 2 + 2 * R * N * O


def tile_list_gatedtwins_bank_store_plain_kernel(
    tc, xt_words, xt_scales, xo_words, xo_scales, w_words, w_scales, w0_words, w0_scales,
    sa, sb, sg, bg, sh, bh, vs_words, vs_scales, offs, offs2, offs3, offs4, offs5, offs6, offs7, out,
):
    nc = tc.nc
    with ExitStack() as ctx:
        keep = ctx.enter_context(tc.tile_pool(name="keep", bufs=1))
        psum = ctx.enter_context(tc.psum_pool(name="psum", bufs=1))

        def new(name, shape, dtype, tag=None):
            return keep.tile(shape, dtype, name=name, tag=tag or name, align_bytes=64)

        def load_list(name, src):
            lst = new(name, list(src.shape), U16)
            nc.sync.dma_start(lst[:], src)
            return lst

        def zero_plane(name, width, engine):
            plane = new(name, [P, width], U8)
            engine.memset(plane[:].bitcast(I32), 0)
            return plane

        def load_plane(plane, scales, queue):
            rows = scales[0].bitcast(I32)
            for q in range(QUADS):
                queue.dma_start(plane[:].bitcast(I32)[32 * q : 32 * q + 4, :], rows[4 * q : 4 * q + 4, :])

        def load_rows(plane, scales, quads):
            rows = scales[0].bitcast(I32)
            for q in quads:
                nc.sync.dma_start(plane[:].bitcast(I32)[32 * q : 32 * q + 4, :], rows[4 * q : 4 * q + 4, :])

        def deal_scales(t):
            dealt = new(f"w_sc{t}", [P, 2, P], U8)
            nc.vector.tensor_copy(dealt[:], w_plane.rearrange("p (s q t) -> p s q t", s=2, t=PACK)[:, :, :, t])
            return dealt

        def load_stage(name, scales, queue):
            stage = new(name, [4, QUADS, scales.shape[2] // 4], I32)
            queue.dma_start(stage[:], scales[0].bitcast(I32).rearrange("(q r) n -> r q n", r=4))
            return stage

        def spread(plane, stage):
            for q in range(QUADS):
                nc.vector.tensor_copy(plane[:].bitcast(I32)[32 * q : 32 * q + 4, :], stage[:, q, :])

        def load_w_stage(queue):
            for s, scales in enumerate((w_scales, w0_scales)):
                queue.dma_start(
                    w_stage_words[0:4, :, s * (R // 4) : (s + 1) * (R // 4)],
                    scales[0].bitcast(I32).rearrange("(q r) n -> r q n", r=4),
                )

        def load_vector(name, src, queue):
            vec = new(name, [P, PACK], F32)
            queue.dma_start(vec[:], src.rearrange("(p t) o -> p (t o)", t=PACK))
            return vec

        def load_words(name, src, dtype, queue):
            tab = new(name, [P, src.shape[2] if dtype != U16 else src.shape[2] // 2], dtype)
            flat = src[0] if dtype == U16 else src[0].rearrange("p n t -> p (n t)")
            queue.dma_start(tab[:].bitcast(I32), flat.bitcast(I32))
            return tab

        def gather(name, window, lst, dtype, count):
            got = new(name, [P, count], dtype)
            nc.vector.tensor_copy(got[:], window.indirect(lst[:]))
            return got

        def clock(name, src):
            tick = new(name, [P, 1], src.dtype)
            nc.gpsimd.tensor_copy(tick[:], src)

        warm = new("warm", [P, 2], F32)
        nc.gpsimd.memset(warm[:, 0:1], 0.0)
        nc.scalar.activation(warm[:, 1:2], warm[:, 0:1], ACT.Sigmoid)
        w_stage = new("w_stage", [P, QUADS, 2 * R], U8)
        w_stage_words = w_stage[:].bitcast(I32)
        nc.vector.memset(w_stage_words[:, 0, :], 0)
        w_plane = w_stage[:, 0, :]
        xo_plane = zero_plane("xo_plane", T, nc.vector)
        xt_plane = zero_plane("xt_plane", T, nc.vector)
        vs_plane = zero_plane("vs_plane", T, nc.vector)
        w_tab = load_words("w_tab", w_words, U16, nc.gpsimd)
        w0_tab = load_words("w0_tab", w0_words, U32, nc.gpsimd)
        l2 = load_list("l2", offs2)
        l1 = load_list("l1", offs)
        xo_tab = load_words("xo_tab", xo_words, U16, nc.sync)
        load_w_stage(nc.sync)
        load_rows(xo_plane, xo_scales, (0, 1))
        xt_tab = load_words("xt_tab", xt_words, U32, nc.sync)
        load_rows(xo_plane, xo_scales, (2, 3))
        load_plane(xt_plane, xt_scales, nc.sync)

        l4 = load_list("l4", offs4)
        sg_t = load_vector("sg_t", sg, nc.sync)
        bg_t = load_vector("bg_t", bg, nc.sync)
        l3 = load_list("l3", offs3)
        sa_t = load_vector("sa_t", sa, nc.sync)
        l6 = load_list("l6", offs6)
        sh_t = load_vector("sh_t", sh, nc.sync)
        bh_t = load_vector("bh_t", bh, nc.sync)
        l5 = load_list("l5", offs5)
        sb_t = load_vector("sb_t", sb, nc.sync)
        l7 = load_list("l7", offs7)
        load_plane(vs_plane, vs_scales, nc.sync)
        vs_tab = load_words("vs_tab", vs_words, U32, nc.sync)

        w_all = new("w_all", [P, PACK, P], U16)
        nc.scalar.copy(w_all[:], w_tab[:].rearrange("p (q t) -> p t q", t=PACK))
        w0_by_t = w0_tab[:].rearrange("p (q t) -> p t q", t=PACK)
        w0_first = new("w0_first", [P, P], U32)
        nc.scalar.copy(w0_first[:], w0_by_t[:, 0, :])
        w0_rest = new("w0_rest", [P, PACK - 1, P], U32)
        nc.scalar.copy(w0_rest[:], w0_by_t[:, 1:, :])
        w_dealt = [w_all[:, t, :] for t in range(PACK)]
        w0_dealt = [w0_first[:]] + [w0_rest[:, t, :] for t in range(PACK - 1)]
        for q in range(1, QUADS):
            nc.vector.tensor_copy(w_stage_words[32 * q : 32 * q + 4, 0, :], w_stage_words[0:4, q, :])
        w_scs = [deal_scales(0)]
        xo_g = gather("xo_g", xo_tab[:], l2, U16, J)
        xt_g = gather("xt_g", xt_tab[:], l1, U32, J)
        xo_sc = gather("xo_sc", xo_plane[:], l2, U8, J)
        xt_sc = gather("xt_sc", xt_plane[:], l1, U8, J)

        a = []
        for t in range(PACK):
            if t == 1:
                rest = new("w_sc_rest", [P, 2, PACK - 1, P], U8, tag="xt_plane")
                nc.vector.tensor_copy(rest[:], w_plane.rearrange("p (s q t) -> p s t q", s=2, t=PACK)[:, :, 1:, :])
                w_scs.extend(rest[:, :, i, :] for i in range(PACK - 1))
            w_sc = w_scs[t]
            acc = psum.tile([P, J], F32, name=f"acc{t}")
            nc.tensor.matmul_mx(
                out=acc[:], lhsT=w0_dealt[t].bitcast(E5M2), lhsT_scale=w_sc[:, 1, :],
                rhs=xo_g[:].bitcast(E2M1), rhs_scale=xo_sc[:], start=True, stop=False,
            )
            nc.tensor.matmul_mx(
                out=acc[:], lhsT=w_dealt[t].bitcast(E2M1), lhsT_scale=w_sc[:, 0, :],
                rhs=xt_g[:].bitcast(E4M3), rhs_scale=xt_sc[:], start=False, stop=True,
            )
            a_t = new(f"a{t}", [P, J], F32)
            nc.vector.tensor_copy(a_t[:], acc[:])
            a.append(a_t)

        vs_sc = gather("vs_sc", vs_plane[:], l7, U8, N)
        vs_g = gather("vs_g", vs_tab[:], l7, U32, N)

        diff = new("diff", [P, PACK, O], F32)
        u_all = new("u_all", [P, PACK, 2, O], F32, tag="vs_tab")
        looks = ((l4, sg_t, bg_t, l3, sa_t), (l6, sh_t, bh_t, l5, sb_t))
        for t in range(PACK):
            col = slice(t, t + 1)
            gates = new(f"gates{t}", [P, 2, O], F32)
            vals = new(f"vals{t}", [P, 2, O], F32)
            for h, (lg, slope, offset, lv, weight) in enumerate(looks):
                nc.scalar.activation(gates[:, h, :], a[t][:].indirect(lg[:]), ACT.Sigmoid, bias=offset[:, col], scale=slope[:, col])
                nc.scalar.activation(vals[:, h, :], a[t][:].indirect(lv[:]), ACT.Copy, scale=weight[:, col])
            u = u_all[:, t]
            if t < PACK - 1:
                nc.vector.tensor_tensor(u, vals[:], gates[:], ALU.mult)
            else:
                for h in range(2):
                    nc.vector.tensor_tensor(u[:, h, :], vals[:, h, :], gates[:, h, :], ALU.mult)
            nc.vector.tensor_tensor(diff[:, t, :], u[:, 0, :], u[:, 1, :], ALU.subtract)

        hid = new("hid", [P, O, PACK], BF16)
        woven = diff[:].rearrange("p t o -> p o t")
        half = O // 2
        nc.vector.scalar_tensor_tensor(hid[:, :half, :], woven[:, :half, :], -1.0, woven[:, :half, :], ALU.mult, ALU.max)
        nc.scalar.activation(hid[:, half:, :], woven[:, half:, :], ACT.Abs)
        hid_codes = new("hid_codes", [P, O], U32)
        hid_sc = new("hid_sc", [P, O], U8)
        nc.vector.quantize_mx(out=hid_codes[:].bitcast(E4M3), scales=hid_sc[:], in_=hid[:].rearrange("p o t -> p (o t)"))


        for h, (copy, queue) in enumerate(((nc.vector.tensor_copy, nc.sync), (nc.scalar.copy, nc.scalar))):
            cols = slice(h * P, (h + 1) * P)
            y = psum.tile([P, O], F32, name=f"y{h}")
            nc.tensor.matmul_mx(
                out=y[:], lhsT=vs_g[:, cols].bitcast(E5M2), lhsT_scale=vs_sc[:, cols],
                rhs=hid_codes[:].bitcast(E4M3), rhs_scale=hid_sc[:], start=True, stop=True,
            )
            y_sb = new(f"y_sb{h}", [P, O], F32)
            copy(y_sb[:], y[:])
            queue.dma_start(out[cols, :], y_sb[:])
